import numpy as np
import ml_dtypes


def mxq(x, axis, fmt="e4m3"):
    dtype, down = {"e4m3": (ml_dtypes.float8_e4m3fn, 7), "e5m2": (ml_dtypes.float8_e5m2, 14)}[fmt]
    v = np.moveaxis(np.asarray(x, np.float32).astype(ml_dtypes.bfloat16).astype(np.float64), axis, -1)
    blocks = v.reshape(v.shape[:-1] + (-1, 32))
    amax = np.abs(blocks).max(-1, keepdims=True)
    byte = np.maximum(np.where(amax > 0, np.frexp(amax)[1] - 1 + 127, 0) - down, 1)
    scale = np.exp2(byte - 127.0)
    codes = (blocks / scale).astype(np.float32).astype(dtype).astype(np.float64)
    return np.moveaxis((codes * scale).reshape(v.shape), -1, axis)


WIDE = False


def mx_kscale(k):
    if not WIDE:
        return np.ones(k)
    levels = np.array([10, -10, 5, -5, 0])
    if k % 512:
        return np.exp2(np.random.permutation(np.resize(levels, k // 32))).repeat(32)
    a = np.empty((k // 512, 16))
    for p in range(k // 512):
        a[p, :8] = np.random.permutation(np.resize(levels, 8))
        for g in range(8):
            far = levels[np.abs(levels - a[p, g]) >= 10]
            a[p, g + 8] = far[np.random.randint(len(far))]
    return np.exp2(a.ravel()).repeat(32)


BF16 = ml_dtypes.bfloat16


def bf(x):
    return np.asarray(x, np.float32).astype(BF16)


def f64(x):
    return np.asarray(x).astype(np.float64)


E2M1 = np.array([0.0, 0.5, 1.0, 1.5, 2.0, 3.0, 4.0, 6.0, -0.0, -0.5, -1.0, -1.5, -2.0, -3.0, -4.0, -6.0])


def pack_weight(w, fmt):
    k, n = w.shape
    w = f64(bf(w)).reshape(k // 32, 32, n)
    amax = np.abs(w).max(1)
    if fmt == "e4m3":
        byte = np.frexp(amax)[1] - 1 + 127 - 7
    else:
        mant, ex = np.frexp(amax / 6.0)
        byte = np.where(mant > 0.5, ex, ex - 1) + 127
    byte = np.clip(np.where(amax > 0, byte, 1), 1, 254)
    scaled = (w * np.exp2(127.0 - byte)[:, None, :]).reshape(k, n).astype(np.float32)
    by_word = np.ascontiguousarray(scaled.reshape(k // 512, 128, 4, n).transpose(0, 1, 3, 2))
    if fmt == "e4m3":
        words = by_word.astype(ml_dtypes.float8_e4m3fn).view(np.uint8)
    else:
        c = by_word.astype(ml_dtypes.float4_e2m1fn).view(np.uint8) & 0xF
        words = c[..., 0::2] | (c[..., 1::2] << 4)
    return np.ascontiguousarray(words), np.ascontiguousarray(byte.astype(np.uint8).reshape(k // 512, 16, n))


def unpack_weight(words, scales, fmt):
    g, p, n, _ = words.shape
    if fmt == "e4m3":
        vals = np.ascontiguousarray(words).view(ml_dtypes.float8_e4m3fn).astype(np.float64)
    else:
        nib = np.empty((g, p, n, 4), np.uint8)
        nib[..., 0::2] = words & 0xF
        nib[..., 1::2] = words >> 4
        vals = E2M1[nib]
    vals = vals * np.repeat(np.exp2(scales.astype(np.float64) - 127.0), 8, axis=1)[..., None]
    return vals.transpose(0, 1, 3, 2).reshape(g * 512, n)
def pack4(w):
    words, scales = pack_weight(w, "e2m1")
    return words.reshape(words.shape[0], 128, -1), scales


def unpack4(words, scales):
    return unpack_weight(words.reshape(words.shape[0], 128, -1, 2), scales, "e2m1")


M, K, N = 1024, 1536, 1024

EPS = 0.1


def setup_inputs():
    s, t = mx_kscale(K), mx_kscale(N)
    m = 0.5 * np.random.standard_normal(K)
    w_old = np.random.standard_normal((K, N)) / np.sqrt(K) / N ** 0.25
    drift = np.random.standard_normal((K, N)) / np.sqrt(K) / N ** 0.25
    w_new = 0.8 * w_old + 0.6 * drift
    words, scales = pack4(w_old / s[:, None] * t)
    return {"x": bf((np.random.standard_normal((M, K)) + m) * s),
            "w_old_words": words,
            "w_old_scales": scales,
            "w_new": bf(w_new / s[:, None] / t),
            "mean_old": bf((m[:, None] * w_old).sum(axis=0) * t),
            "mean_new": bf((m[:, None] * w_new).sum(axis=0) / t)}


def reference(x, w_old_words, w_old_scales, w_new, mean_old, mean_new):
    xq = mxq(f64(x), 1, "e4m3")
    a = (xq @ unpack4(w_old_words, w_old_scales)) - f64(mean_old)
    b = (xq @ mxq(f64(w_new), 0, "e4m3")) - f64(mean_new)
    gram = mxq(a, 1, "e4m3") @ mxq(b, 1, "e4m3").T
    return gram * (1.0 + EPS * np.eye(M))

@@ -1,0 +1,332 @@
+from contextlib import ExitStack
+
+import concourse.mybir as mybir
+from concourse.masks import make_identity
+
+M, K, N = 1024, 1536, 1024
+EPS = 0.1
+FLOPS = 2 * (2 * M * K * N) + 2 * M * M * N
+
+F32 = mybir.dt.float32
+BF16 = mybir.dt.bfloat16
+I32 = mybir.dt.int32
+U32 = mybir.dt.uint32
+U8 = mybir.dt.uint8
+FP8X4 = mybir.dt.float8_e4m3fn_x4
+FP4X4 = mybir.dt.float4_e2m1fn_x4
+ALU = mybir.AluOpType
+ACT = mybir.ActivationFunctionType
+
+P = 128
+PACK = 4
+PASS = P * PACK
+KP = K // PASS
+NP = N // PASS
+HALF = 512
+OLD, NEW = 0, 1
+
+
+def tile_two_snapshot_sample_gram_s11_kernel(tc, x, w_old_words, w_old_scales, w_new, mean_old, mean_new, out):
+    nc = tc.nc
+    with ExitStack() as ctx:
+        keep = ctx.enter_context(tc.tile_pool(name="keep", bufs=1))
+        ring = ctx.enter_context(tc.tile_pool(name="ring", bufs=3))
+        psum = ctx.enter_context(tc.psum_pool(name="psum", bufs=1))
+        ctx.enter_context(tc.manual_schedule())
+
+        def kept(name, shape, dtype):
+            return keep.tile(shape, dtype, name=name, tag=name, align_bytes=64)
+
+        def bank(b):
+            return psum.tile([P, HALF], F32, name="bank%d" % b, tag="bank%d" % b)
+
+        def mx_pair(name):
+            return kept(name + "_codes", [P, HALF], U32), kept(name + "_scales", [P, HALF], U8)
+
+        def quantize(pair, grouped):
+            nc.vector.quantize_mx(out=pair[0][:].bitcast(FP8X4), scales=pair[1][:], in_=grouped[:])
+
+        ident = kept("ident", [P, P], F32)
+        make_identity(nc, ident[:])
+        mean_rows = kept("mean_rows", [2 * PACK, NP * P], BF16)
+        for s, mean in ((OLD, mean_old), (NEW, mean_new)):
+            nc.gpsimd.dma_start(
+                out=mean_rows[PACK * s : PACK * (s + 1), :].rearrange("t (a r) -> t a r", r=4),
+                in_=mean.rearrange("(a t r) -> t a r", t=PACK, r=4),
+            )
+        neg_rows = kept("neg_rows", [P, NP * P], F32)
+        nc.gpsimd.memset(neg_rows[:], 0.0)
+        shift = kept("shift", [P, 2 * HALF - P], F32)
+        nc.gpsimd.memset(shift[:], 1.0)
+        nc.gpsimd.tensor_scalar(out=neg_rows[0 : 2 * PACK, :], in0=mean_rows[:], scalar1=-1.0, scalar2=0.0, op0=ALU.mult, op1=ALU.add)
+        nc.scalar.activation(out=shift[:, HALF - P : HALF], in_=ident[:], func=ACT.Identity, bias=shift[:, 0:1], scale=EPS)
+
+        x_raw = {}
+
+        def load_x(h, g, parts):
+            tiles = HALF // P // parts
+            for part in range(parts):
+                t = kept("x_raw_%d_%d_%d" % (h, g, part), [P, tiles, PASS], BF16)
+                r0 = h * HALF + part * tiles * P
+                nc.sync.dma_start(out=t[:], in_=x[r0 : r0 + tiles * P, g * PASS : (g + 1) * PASS].rearrange("(a p) k -> p a k", p=P))
+                for a in range(tiles):
+                    x_raw[(h, g, part * tiles + a)] = t[:].rearrange("p a k -> p (a k)").bitcast(F32)[:, a * 2 * P : (a + 1) * 2 * P]
+
+        wo_raw = {}
+
+        def load_w_old(g):
+            wo_raw[g] = kept("wo_raw_%d" % g, [P, N // 2], I32)
+            nc.sync.dma_start(out=wo_raw[g][:], in_=w_old_words[g].bitcast(I32))
+
+        so_raw = kept("so_raw", [P, KP * N // 4], I32)
+        nc.vector.memset(so_raw[:], 0)
+
+        def load_scales_old():
+            for q in range(4):
+                nc.sync.dma_start(
+                    out=so_raw[32 * q : 32 * q + 4, :].rearrange("r (g w) -> r g w", g=KP),
+                    in_=w_old_scales[:, 4 * q : 4 * q + 4, :].bitcast(I32).rearrange("g r w -> r g w"),
+                )
+
+        wn_raw = {}
+
+        def load_w_new(c, g):
+            wn_raw[(c, g)] = kept("wn_raw_%d_%d" % (c, g), [P, PACK, PASS], BF16)
+            nc.sync.dma_start(
+                out=wn_raw[(c, g)][:],
+                in_=w_new[g * PASS : (g + 1) * PASS, c * PASS : (c + 1) * PASS].rearrange("(p j) n -> p j n", j=PACK),
+            )
+
+        load_x(0, 0, 2)
+        load_w_old(0)
+        load_scales_old()
+        load_x(0, 1, 1)
+        load_w_old(1)
+        load_x(0, 2, 1)
+        load_w_old(2)
+        for g in range(KP):
+            load_w_new(0, g)
+            load_x(1, g, 1)
+        for g in range(KP):
+            load_w_new(1, g)
+
+        wo_codes = {}
+
+        def sort_w_old(g):
+            wo_codes[g] = kept("wo_codes_%d" % g, [P, 2 * N], U8)
+            nc.vector.tensor_copy(
+                out=wo_codes[g][:].bitcast(I32).rearrange("p (c t a w) -> p c t a w", c=NP, t=PACK, w=2),
+                in_=wo_raw[g][:].rearrange("p (c a t w) -> p c t a w", c=NP, t=PACK, w=2),
+            )
+
+        wo_scales = kept("wo_scales", [P, KP * N], U8)
+
+        def sort_scales_old():
+            nc.vector.tensor_copy(
+                out=wo_scales[:].bitcast(I32).rearrange("p (b t a) -> p b t a", b=KP * NP, t=PACK),
+                in_=so_raw[:].rearrange("p (b a t) -> p b t a", b=KP * NP, t=PACK),
+            )
+
+        x_grouped = {}
+        xq = {}
+
+        def turn_x(h, g, banks):
+            x_grouped[(h, g)] = ring.tile([P, HALF * PACK], BF16, name="x_grouped", tag="x_grouped", align_bytes=64)
+            words = x_grouped[(h, g)][:].bitcast(F32)
+            for pair, b in enumerate(banks):
+                ps = bank(b)
+                for a in range(2):
+                    for u in range(2):
+                        col = (2 * a + u) * P
+                        nc.tensor.transpose(ps[:, col : col + P], x_raw[(h, g, 2 * pair + a)][:, u : 2 * P : 2], ident[:])
+                nc.scalar.copy(
+                    out=words[:, pair * HALF : (pair + 1) * HALF].rearrange("p (a r u) -> p a r u", a=2, u=2),
+                    in_=ps[:].rearrange("p (a u r) -> p a r u", a=2, u=2),
+                )
+
+        def quant_x(h, g):
+            xq[(h, g)] = mx_pair("xq_%d_%d" % (h, g))
+            quantize(xq[(h, g)], x_grouped[(h, g)])
+
+        neg_mean = kept("neg_mean", [P, NP, 2 * PACK], F32)
+
+        def turn_means(b):
+            ps = bank(b)
+            for c in range(NP):
+                nc.tensor.transpose(ps[:, c * P : (c + 1) * P], neg_rows[:, c * P : (c + 1) * P], ident[:])
+            nc.scalar.copy(out=neg_mean[:], in_=ps[:, 0 : NP * P].rearrange("p (c r) -> p c r", c=NP)[:, :, 0 : 2 * PACK])
+
+        grouped = {}
+        quantized = {}
+
+        def new_grouped(key):
+            grouped[key] = ring.tile([P, HALF * PACK], BF16, name="grouped", tag="grouped", align_bytes=64)
+            return grouped[key]
+
+        def group_w(c, g):
+            dst = new_grouped(("w", c, g))
+            nc.vector.tensor_copy(
+                out=dst[:].rearrange("p (t a r j) -> p a t j r", t=PACK, r=4, j=PACK),
+                in_=wn_raw[(c, g)][:].rearrange("p j (a t r) -> p a t j r", t=PACK, r=4),
+            )
+
+        def quant(key):
+            quantized[key] = mx_pair("q_%s_%d_%d" % (key[0], key[1], key[2]))
+            quantize(quantized[key], grouped[key])
+
+        open_banks = {}
+        centred = {}
+
+        def stage1_pass(s, h, c, t, g, b):
+            if g == 0:
+                open_banks[b] = bank(b)
+            cols = slice(t * P, (t + 1) * P)
+            if s == OLD:
+                c0 = c * PASS + t * P
+                lhsT = wo_codes[g][:, 2 * c0 : 2 * (c0 + P)].bitcast(FP4X4)
+                lhsT_scale = wo_scales[:, g * N + c0 : g * N + c0 + P]
+            else:
+                lhsT = quantized[("w", c, g)][0][:, cols].bitcast(FP8X4)
+                lhsT_scale = quantized[("w", c, g)][1][:, cols]
+            nc.tensor.matmul_mx(
+                out=open_banks[b][:], lhsT=lhsT, lhsT_scale=lhsT_scale,
+                rhs=xq[(h, g)][0][:].bitcast(FP8X4), rhs_scale=xq[(h, g)][1][:],
+                start=(g == 0), stop=(g == KP - 1),
+            )
+            if g == KP - 1:
+                if t == 0:
+                    centred[(s, h, c)] = kept("centred_%d_%d_%d" % (s, h, c), [P, PACK, HALF], BF16)
+                nc.scalar.activation(
+                    out=centred[(s, h, c)][:, t, :], in_=open_banks[b][:], func=ACT.Identity,
+                    bias=neg_mean[:, c, PACK * s + t : PACK * s + t + 1], scale=1.0,
+                )
+
+        def stage1_by_pass(s, h, c, g, b0):
+            for t in range(PACK):
+                stage1_pass(s, h, c, t, g, b0 + t)
+
+        def stage1_by_slot(s, h, c, slots, b0):
+            for i, t in enumerate(slots):
+                for g in range(KP):
+                    stage1_pass(s, h, c, t, g, b0 + i)
+
+        def group_ab(s, h, c):
+            dst = new_grouped(("ab"[s], h, c))
+            nc.vector.tensor_copy(
+                out=dst[:].rearrange("p (a i t) -> p a t i", i=4, t=PACK),
+                in_=centred[(s, h, c)][:].rearrange("p t (a i) -> p a t i", i=4),
+            )
+
+        def gram_pass(i, h, c, b):
+            if c == 0:
+                open_banks[b] = bank(b)
+            a_codes, a_scales = quantized[("a", i // 4, c)]
+            b_codes, b_scales = quantized[("b", h, c)]
+            cols = slice((i % 4) * P, (i % 4 + 1) * P)
+            nc.tensor.matmul_mx(
+                out=open_banks[b][:], lhsT=a_codes[:, cols].bitcast(FP8X4), lhsT_scale=a_scales[:, cols],
+                rhs=b_codes[:].bitcast(FP8X4), rhs_scale=b_scales[:],
+                start=(c == 0), stop=(c == NP - 1),
+            )
+
+        result = {}
+
+        def store(i, h):
+            nc.sync.dma_start(out=out[i * P : (i + 1) * P, h * HALF : (h + 1) * HALF], in_=result[(i, h)][:])
+
+        def copy_out(i, h, b):
+            result[(i, h)] = kept("result_%d_%d" % (i, h), [P, HALF], F32)
+            nc.scalar.copy(out=result[(i, h)][:], in_=open_banks[b][:])
+
+        def shift_in_place(i, h):
+            cols = slice((i % 4) * P, (i % 4 + 1) * P)
+            nc.vector.tensor_tensor(out=result[(i, h)][:, cols], in0=result[(i, h)][:, cols], in1=shift[:, HALF - P : HALF], op=ALU.mult)
+
+        def shifted_out(i, h, b):
+            result[(i, h)] = kept("result_%d_%d" % (i, h), [P, HALF], F32)
+            c0 = HALF - P - (i % 4) * P
+            nc.vector.tensor_tensor(out=result[(i, h)][:], in0=open_banks[b][:], in1=shift[:, c0 : c0 + HALF], op=ALU.mult)
+
+        turn_x(0, 0, (0, 1))
+        sort_w_old(0)
+        sort_scales_old()
+        quant_x(0, 0)
+        turn_x(0, 1, (2, 3))
+        stage1_by_pass(OLD, 0, 0, 0, 4)
+        sort_w_old(1)
+        quant_x(0, 1)
+        turn_x(0, 2, (0, 1))
+        stage1_by_pass(OLD, 0, 0, 1, 4)
+        sort_w_old(2)
+        quant_x(0, 2)
+        turn_means(0)
+        turn_x(1, 0, (2, 3))
+        stage1_by_pass(OLD, 0, 0, 2, 4)
+        group_w(0, 0)
+        quant_x(1, 0)
+        quant(("w", 0, 0))
+        stage1_by_slot(OLD, 0, 1, (0, 1), 0)
+        turn_x(1, 1, (2, 3))
+        group_w(0, 1)
+        group_w(0, 2)
+        quant(("w", 0, 1))
+        quant_x(1, 1)
+        quant(("w", 0, 2))
+        stage1_by_slot(OLD, 0, 1, (2, 3), 4)
+        turn_x(1, 2, (6, 7))
+        group_w(1, 0)
+        quant_x(1, 2)
+        for g in range(KP):
+            stage1_by_pass(OLD, 1, 0, g, 0)
+        group_w(1, 1)
+        quant(("w", 1, 0))
+        group_w(1, 2)
+        quant(("w", 1, 1))
+        group_ab(OLD, 0, 0)
+        quant(("w", 1, 2))
+        stage1_by_slot(OLD, 1, 1, range(PACK), 4)
+        group_ab(OLD, 0, 1)
+        quant(("a", 0, 0))
+        stage1_by_slot(NEW, 0, 0, range(PACK), 0)
+        group_ab(OLD, 1, 0)
+        quant(("a", 0, 1))
+        group_ab(NEW, 0, 0)
+        quant(("a", 1, 0))
+        stage1_by_slot(NEW, 0, 1, range(PACK), 4)
+        group_ab(OLD, 1, 1)
+        quant(("b", 0, 0))
+        group_ab(NEW, 0, 1)
+        quant(("a", 1, 1))
+        quant(("b", 0, 1))
+        stage1_by_slot(NEW, 1, 0, range(PACK), 0)
+        for i in range(4):
+            for c in range(NP):
+                gram_pass(i, 0, c, 4 + i)
+            copy_out(i, 0, 4 + i)
+        group_ab(NEW, 1, 0)
+        shift_in_place(0, 0)
+        store(0, 0)
+        quant(("b", 1, 0))
+        for i in range(1, 4):
+            shift_in_place(i, 0)
+            store(i, 0)
+        stage1_by_slot(NEW, 1, 1, range(PACK), 0)
+        group_ab(NEW, 1, 1)
+        quant(("b", 1, 1))
+        for i in range(4, 8):
+            for c in range(NP):
+                gram_pass(i, 0, c, i)
+            copy_out(i, 0, i)
+            store(i, 0)
+        first = (4, 0, 5, 1)
+        for b, i in enumerate(first):
+            gram_pass(i, 1, 0, b)
+        for b, i in enumerate(first + (6, 2, 7, 3)):
+            if b >= 4:
+                gram_pass(i, 1, 0, b)
+            gram_pass(i, 1, 1, b)
+            if i >= 4:
+                shifted_out(i, 1, b)
+            else:
+                copy_out(i, 1, b)
+            store(i, 1)

@@ -48,29 +48,21 @@ def tile_two_snapshot_sample_gram_s11_kernel(tc, x, w_old_words, w_old_scales, w
 
         ident = kept("ident", [P, P], F32)
         make_identity(nc, ident[:])
-        mean_rows = kept("mean_rows", [2 * PACK, NP * P], BF16)
-        for s, mean in ((OLD, mean_old), (NEW, mean_new)):
-            nc.gpsimd.dma_start(
-                out=mean_rows[PACK * s : PACK * (s + 1), :].rearrange("t (a r) -> t a r", r=4),
-                in_=mean.rearrange("(a t r) -> t a r", t=PACK, r=4),
-            )
-        neg_rows = kept("neg_rows", [P, NP * P], F32)
-        nc.gpsimd.memset(neg_rows[:], 0.0)
         shift = kept("shift", [P, 2 * HALF - P], F32)
         nc.gpsimd.memset(shift[:], 1.0)
-        nc.gpsimd.tensor_scalar(out=neg_rows[0 : 2 * PACK, :], in0=mean_rows[:], scalar1=-1.0, scalar2=0.0, op0=ALU.mult, op1=ALU.add)
+        neg_rows = kept("neg_rows", [P, PASS], F32)
+        nc.vector.memset(neg_rows[:], 0.0)
+        mean_rows = kept("mean_rows", [2 * NP, PASS], BF16)
+        for s, mean in ((OLD, mean_old), (NEW, mean_new)):
+            nc.scalar.dma_start(out=mean_rows[NP * s : NP * (s + 1), :], in_=mean.rearrange("(c n) -> c n", c=NP))
         nc.scalar.activation(out=shift[:, HALF - P : HALF], in_=ident[:], func=ACT.Identity, bias=shift[:, 0:1], scale=EPS)
 
-        x_raw = {}
+        x_words = {}
 
-        def load_x(h, g, parts):
-            tiles = HALF // P // parts
-            for part in range(parts):
-                t = kept("x_raw_%d_%d_%d" % (h, g, part), [P, tiles, PASS], BF16)
-                r0 = h * HALF + part * tiles * P
-                nc.sync.dma_start(out=t[:], in_=x[r0 : r0 + tiles * P, g * PASS : (g + 1) * PASS].rearrange("(a p) k -> p a k", p=P))
-                for a in range(tiles):
-                    x_raw[(h, g, part * tiles + a)] = t[:].rearrange("p a k -> p (a k)").bitcast(F32)[:, a * 2 * P : (a + 1) * 2 * P]
+        def load_x(i):
+            t = kept("x_raw_%d" % i, [P, K], BF16)
+            nc.sync.dma_start(out=t[:], in_=x[i * P : (i + 1) * P, :])
+            x_words[i] = t[:].bitcast(F32)
 
         wo_raw = {}
 
@@ -82,33 +74,29 @@ def tile_two_snapshot_sample_gram_s11_kernel(tc, x, w_old_words, w_old_scales, w
         nc.vector.memset(so_raw[:], 0)
 
         def load_scales_old():
-            for q in range(4):
+            for r in range(4):
                 nc.sync.dma_start(
-                    out=so_raw[32 * q : 32 * q + 4, :].rearrange("r (g w) -> r g w", g=KP),
-                    in_=w_old_scales[:, 4 * q : 4 * q + 4, :].bitcast(I32).rearrange("g r w -> r g w"),
+                    out=so_raw[r:P:32, :].rearrange("q (g w) -> q g w", g=KP),
+                    in_=w_old_scales.bitcast(I32)[:, r:16:4, :].rearrange("g q w -> q g w"),
                 )
 
         wn_raw = {}
 
-        def load_w_new(c, g):
-            wn_raw[(c, g)] = kept("wn_raw_%d_%d" % (c, g), [P, PACK, PASS], BF16)
-            nc.sync.dma_start(
-                out=wn_raw[(c, g)][:],
-                in_=w_new[g * PASS : (g + 1) * PASS, c * PASS : (c + 1) * PASS].rearrange("(p j) n -> p j n", j=PACK),
-            )
+        def load_w_new(g):
+            wn_raw[g] = kept("wn_raw_%d" % g, [P, PACK, N], BF16)
+            nc.sync.dma_start(out=wn_raw[g][:], in_=w_new[g * PASS : (g + 1) * PASS, :].rearrange("(p j) n -> p j n", j=PACK))
 
-        load_x(0, 0, 2)
+        for i in range(4):
+            load_x(i)
         load_w_old(0)
         load_scales_old()
-        load_x(0, 1, 1)
         load_w_old(1)
-        load_x(0, 2, 1)
         load_w_old(2)
-        for g in range(KP):
-            load_w_new(0, g)
-            load_x(1, g, 1)
-        for g in range(KP):
-            load_w_new(1, g)
+        load_w_new(0)
+        for i in range(4, 8):
+            load_x(i)
+        load_w_new(1)
+        load_w_new(2)
 
         wo_codes = {}
 
@@ -121,53 +109,76 @@ def tile_two_snapshot_sample_gram_s11_kernel(tc, x, w_old_words, w_old_scales, w
 
         wo_scales = kept("wo_scales", [P, KP * N], U8)
 
-        def sort_scales_old():
+        def sort_scales_old(g):
             nc.vector.tensor_copy(
-                out=wo_scales[:].bitcast(I32).rearrange("p (b t a) -> p b t a", b=KP * NP, t=PACK),
-                in_=so_raw[:].rearrange("p (b a t) -> p b t a", b=KP * NP, t=PACK),
+                out=wo_scales[:, g * N : (g + 1) * N].bitcast(I32).rearrange("p (c t a) -> p c t a", c=NP, t=PACK),
+                in_=so_raw[:, g * N // 4 : (g + 1) * N // 4].rearrange("p (c a t) -> p c t a", c=NP, t=PACK),
             )
 
         x_grouped = {}
         xq = {}
 
-        def turn_x(h, g, banks):
-            x_grouped[(h, g)] = ring.tile([P, HALF * PACK], BF16, name="x_grouped", tag="x_grouped", align_bytes=64)
-            words = x_grouped[(h, g)][:].bitcast(F32)
-            for pair, b in enumerate(banks):
-                ps = bank(b)
-                for a in range(2):
+        x_sorted = {}
+
+        def sort_x(i):
+            x_sorted[i] = ring.tile([P, K // 2], F32, name="x_sorted", tag="x_sorted", bufs=4, align_bytes=64)
+            nc.vector.tensor_copy(
+                out=x_sorted[i][:].rearrange("p (g u w) -> p g u w", g=KP, u=2),
+                in_=x_words[i].rearrange("p (g w u) -> p g u w", g=KP, u=2),
+            )
+
+        turned = {}
+
+        def turn_x(h, pair, banks):
+            tiles = [bank(b) for b in banks]
+            turned[(h, pair)] = tiles
+            steps = [(a, g) for a in range(2) for g in range(KP)] if pair == 0 else [(a, g) for g in range(KP) for a in range(2)]
+            for a, g in steps:
+                if True:
                     for u in range(2):
                         col = (2 * a + u) * P
-                        nc.tensor.transpose(ps[:, col : col + P], x_raw[(h, g, 2 * pair + a)][:, u : 2 * P : 2], ident[:])
-                nc.scalar.copy(
-                    out=words[:, pair * HALF : (pair + 1) * HALF].rearrange("p (a r u) -> p a r u", a=2, u=2),
-                    in_=ps[:].rearrange("p (a u r) -> p a r u", a=2, u=2),
-                )
+                        i = 4 * h + 2 * pair + a
+                        if i in x_sorted:
+                            src = x_sorted[i][:, (2 * g + u) * P : (2 * g + u + 1) * P]
+                        else:
+                            src = x_words[i][:, g * 2 * P + u : (g + 1) * 2 * P : 2]
+                        nc.tensor.transpose(tiles[g][:, col : col + P], src, ident[:])
+
+        def empty_x(h, pair, g, copy):
+            if pair == 0:
+                x_grouped[(h, g)] = ring.tile([P, HALF * PACK], BF16, name="x_grouped", tag="x_grouped", align_bytes=64)
+            words = x_grouped[(h, g)][:].bitcast(F32)
+            copy(
+                out=words[:, pair * HALF : (pair + 1) * HALF].rearrange("p (a r u) -> p a r u", a=2, u=2),
+                in_=turned[(h, pair)][g][:].rearrange("p (a u r) -> p a r u", a=2, u=2),
+            )
 
         def quant_x(h, g):
             xq[(h, g)] = mx_pair("xq_%d_%d" % (h, g))
             quantize(xq[(h, g)], x_grouped[(h, g)])
 
-        neg_mean = kept("neg_mean", [P, NP, 2 * PACK], F32)
+        neg_mean = kept("neg_mean", [P, PACK, 2 * NP], F32)
 
         def turn_means(b):
             ps = bank(b)
-            for c in range(NP):
-                nc.tensor.transpose(ps[:, c * P : (c + 1) * P], neg_rows[:, c * P : (c + 1) * P], ident[:])
-            nc.scalar.copy(out=neg_mean[:], in_=ps[:, 0 : NP * P].rearrange("p (c r) -> p c r", c=NP)[:, :, 0 : 2 * PACK])
+            for t in range(PACK):
+                nc.tensor.transpose(ps[:, t * P : (t + 1) * P], neg_rows[:, t * P : (t + 1) * P], ident[:])
+            nc.scalar.copy(out=neg_mean[:], in_=ps[:].rearrange("p (t r) -> p t r", t=PACK)[:, :, 0 : 2 * NP])
 
         grouped = {}
         quantized = {}
 
         def new_grouped(key):
-            grouped[key] = ring.tile([P, HALF * PACK], BF16, name="grouped", tag="grouped", align_bytes=64)
+            grouped[key] = ring.tile([P, HALF * PACK], BF16, name="grouped", tag="grouped", bufs=4, align_bytes=64)
             return grouped[key]
 
-        def group_w(c, g):
-            dst = new_grouped(("w", c, g))
-            nc.vector.tensor_copy(
-                out=dst[:].rearrange("p (t a r j) -> p a t j r", t=PACK, r=4, j=PACK),
-                in_=wn_raw[(c, g)][:].rearrange("p j (a t r) -> p a t j r", t=PACK, r=4),
+        def group_w(c, g, part=None, copy=nc.vector.tensor_copy):
+            if part in (None, 0):
+                new_grouped(("w", c, g))
+            cols = slice(0, 32) if part is None else slice(16 * part, 16 * (part + 1))
+            copy(
+                out=grouped[("w", c, g)][:].rearrange("p (t a r j) -> p a t j r", t=PACK, r=4, j=PACK)[:, cols],
+                in_=wn_raw[g][:, :, c * PASS : (c + 1) * PASS].rearrange("p j (a t r) -> p a t j r", t=PACK, r=4)[:, cols],
             )
 
         def quant(key):
@@ -193,26 +204,35 @@ def tile_two_snapshot_sample_gram_s11_kernel(tc, x, w_old_words, w_old_scales, w
                 rhs=xq[(h, g)][0][:].bitcast(FP8X4), rhs_scale=xq[(h, g)][1][:],
                 start=(g == 0), stop=(g == KP - 1),
             )
-            if g == KP - 1:
-                if t == 0:
-                    centred[(s, h, c)] = kept("centred_%d_%d_%d" % (s, h, c), [P, PACK, HALF], BF16)
-                nc.scalar.activation(
-                    out=centred[(s, h, c)][:, t, :], in_=open_banks[b][:], func=ACT.Identity,
-                    bias=neg_mean[:, c, PACK * s + t : PACK * s + t + 1], scale=1.0,
-                )
 
-        def stage1_by_pass(s, h, c, g, b0):
+        def centre(s, h, c, t, b):
+            if t == 0:
+                centred[(s, h, c)] = kept("centred_%d_%d_%d" % (s, h, c), [P, PACK, HALF], BF16)
+            nc.scalar.activation(
+                out=centred[(s, h, c)][:, t, :], in_=open_banks[b][:], func=ACT.Identity,
+                bias=neg_mean[:, t, NP * s + c : NP * s + c + 1], scale=1.0,
+            )
+
+        def stage1_by_pass(s, h, c, g, banks):
             for t in range(PACK):
-                stage1_pass(s, h, c, t, g, b0 + t)
+                stage1_pass(s, h, c, t, g, banks[t])
 
-        def stage1_by_slot(s, h, c, slots, b0):
-            for i, t in enumerate(slots):
-                for g in range(KP):
-                    stage1_pass(s, h, c, t, g, b0 + i)
+        def centre_all(s, h, c, banks):
+            for t in range(PACK):
+                centre(s, h, c, t, banks[t])
 
-        def group_ab(s, h, c):
+        def stage1_slot(s, h, c, t, b):
+            for g in range(KP):
+                stage1_pass(s, h, c, t, g, b)
+
+        def stage1_by_slot(s, h, c, slots, banks):
+            for t, b in zip(slots, banks):
+                stage1_slot(s, h, c, t, b)
+                centre(s, h, c, t, b)
+
+        def group_ab(s, h, c, copy):
             dst = new_grouped(("ab"[s], h, c))
-            nc.vector.tensor_copy(
+            copy(
                 out=dst[:].rearrange("p (a i t) -> p a t i", i=4, t=PACK),
                 in_=centred[(s, h, c)][:].rearrange("p t (a i) -> p a t i", i=4),
             )
@@ -247,86 +267,96 @@ def tile_two_snapshot_sample_gram_s11_kernel(tc, x, w_old_words, w_old_scales, w
             c0 = HALF - P - (i % 4) * P
             nc.vector.tensor_tensor(out=result[(i, h)][:], in0=open_banks[b][:], in1=shift[:, c0 : c0 + HALF], op=ALU.mult)
 
-        turn_x(0, 0, (0, 1))
-        sort_w_old(0)
-        sort_scales_old()
-        quant_x(0, 0)
-        turn_x(0, 1, (2, 3))
-        stage1_by_pass(OLD, 0, 0, 0, 4)
-        sort_w_old(1)
-        quant_x(0, 1)
-        turn_x(0, 2, (0, 1))
-        stage1_by_pass(OLD, 0, 0, 1, 4)
-        sort_w_old(2)
-        quant_x(0, 2)
-        turn_means(0)
-        turn_x(1, 0, (2, 3))
-        stage1_by_pass(OLD, 0, 0, 2, 4)
+        low, high = range(4), range(4, 8)
+        set_x, set_y = (0, 1, 2, 3), (4, 5, 6, 7)
+        on_vector, on_scalar = nc.vector.tensor_copy, nc.scalar.copy
+        turn_x(0, 0, (0, 1, 2))
+        nc.vector.tensor_scalar(
+            out=neg_rows[0 : 2 * NP, :].rearrange("s (t a r) -> s t a r", t=PACK, r=4),
+            in0=mean_rows[:].rearrange("s (a t r) -> s t a r", t=PACK, r=4),
+            scalar1=-1.0, scalar2=None, op0=ALU.mult,
+        )
+        empty_x(0, 0, 0, on_scalar)
+        empty_x(0, 0, 1, on_scalar)
+        empty_x(0, 0, 2, on_vector)
+        turn_x(0, 1, (4, 5, 6))
+        for g in range(KP):
+            empty_x(0, 1, g, on_scalar)
+        turn_means(7)
+        for g in range(KP):
+            sort_w_old(g)
+            sort_scales_old(g)
+            quant_x(0, g)
+            stage1_by_pass(OLD, 0, 0, g, set_x)
+        group_w(1, 0, 0, on_scalar)
+        centre_all(OLD, 0, 0, set_x)
         group_w(0, 0)
-        quant_x(1, 0)
+        sort_x(4)
+        sort_x(5)
+        group_w(1, 0, 1)
+        sort_x(6)
         quant(("w", 0, 0))
-        stage1_by_slot(OLD, 0, 1, (0, 1), 0)
-        turn_x(1, 1, (2, 3))
-        group_w(0, 1)
+        sort_x(7)
+        stage1_by_slot(OLD, 0, 1, (0, 1), (6, 7))
+        quant(("w", 1, 0))
+        turn_x(1, 0, (0, 2, 4))
+        turn_x(1, 1, (1, 3, 5))
+        stage1_slot(OLD, 0, 1, 2, 6)
+        stage1_slot(OLD, 0, 1, 3, 7)
+        group_ab(OLD, 0, 0, on_vector)
+        for g in range(KP):
+            empty_x(1, 0, g, on_scalar)
+            empty_x(1, 1, g, on_scalar)
+        quant(("a", 0, 0))
+        quant_x(1, 0)
+        group_w(0, 1, 0)
+        quant_x(1, 1)
+        group_w(0, 1, 1)
+        quant_x(1, 2)
+        centre(OLD, 0, 1, 2, 6)
+        centre(OLD, 0, 1, 3, 7)
+        for g in range(KP):
+            stage1_by_pass(OLD, 1, 0, g, set_x)
+        group_ab(OLD, 0, 1, on_scalar)
+        centre_all(OLD, 1, 0, set_x)
         group_w(0, 2)
         quant(("w", 0, 1))
-        quant_x(1, 1)
-        quant(("w", 0, 2))
-        stage1_by_slot(OLD, 0, 1, (2, 3), 4)
-        turn_x(1, 2, (6, 7))
-        group_w(1, 0)
-        quant_x(1, 2)
-        for g in range(KP):
-            stage1_by_pass(OLD, 1, 0, g, 0)
         group_w(1, 1)
-        quant(("w", 1, 0))
+        quant(("w", 0, 2))
         group_w(1, 2)
         quant(("w", 1, 1))
-        group_ab(OLD, 0, 0)
         quant(("w", 1, 2))
-        stage1_by_slot(OLD, 1, 1, range(PACK), 4)
-        group_ab(OLD, 0, 1)
-        quant(("a", 0, 0))
-        stage1_by_slot(NEW, 0, 0, range(PACK), 0)
-        group_ab(OLD, 1, 0)
         quant(("a", 0, 1))
-        group_ab(NEW, 0, 0)
+        stage1_by_slot(OLD, 1, 1, low, set_y)
+        group_ab(OLD, 1, 0, on_vector)
+        stage1_by_slot(NEW, 0, 0, low, set_x)
+        group_ab(OLD, 1, 1, on_vector)
         quant(("a", 1, 0))
-        stage1_by_slot(NEW, 0, 1, range(PACK), 4)
-        group_ab(OLD, 1, 1)
-        quant(("b", 0, 0))
-        group_ab(NEW, 0, 1)
+        group_ab(NEW, 0, 0, on_vector)
         quant(("a", 1, 1))
+        quant(("b", 0, 0))
+        stage1_by_slot(NEW, 0, 1, low, set_y)
+        group_ab(NEW, 0, 1, on_vector)
         quant(("b", 0, 1))
-        stage1_by_slot(NEW, 1, 0, range(PACK), 0)
-        for i in range(4):
-            for c in range(NP):
-                gram_pass(i, 0, c, 4 + i)
-            copy_out(i, 0, 4 + i)
-        group_ab(NEW, 1, 0)
-        shift_in_place(0, 0)
-        store(0, 0)
+        stage1_by_slot(NEW, 1, 0, low, set_x)
+        group_ab(NEW, 1, 0, on_vector)
         quant(("b", 1, 0))
-        for i in range(1, 4):
-            shift_in_place(i, 0)
-            store(i, 0)
-        stage1_by_slot(NEW, 1, 1, range(PACK), 0)
-        group_ab(NEW, 1, 1)
-        quant(("b", 1, 1))
-        for i in range(4, 8):
+        order = [(4, 0), (5, 0), (6, 0), (7, 0), (0, 0), (1, 0), (2, 0), (3, 0), (4, 1), (5, 1), (0, 1), (6, 1), (1, 1), (7, 1), (2, 1), (3, 1)]
+        banks = list(range(8)) * 2
+
+        def gram(step):
+            i, h = order[step]
+            b = banks[step]
             for c in range(NP):
-                gram_pass(i, 0, c, i)
-            copy_out(i, 0, i)
-            store(i, 0)
-        first = (4, 0, 5, 1)
-        for b, i in enumerate(first):
-            gram_pass(i, 1, 0, b)
-        for b, i in enumerate(first + (6, 2, 7, 3)):
-            if b >= 4:
-                gram_pass(i, 1, 0, b)
-            gram_pass(i, 1, 1, b)
-            if i >= 4:
-                shifted_out(i, 1, b)
+                gram_pass(i, h, c, b)
+            if i // 4 == h:
+                shifted_out(i, h, b)
             else:
-                copy_out(i, 1, b)
-            store(i, 1)
+                copy_out(i, h, b)
+            store(i, h)
+
+        stage1_by_slot(NEW, 1, 1, low, set_y)
+        group_ab(NEW, 1, 1, on_vector)
+        quant(("b", 1, 1))
+        for step in range(16):
+            gram(step)

@@ -92,9 +92,9 @@ def tile_two_snapshot_sample_gram_s11_kernel(tc, x, w_old_words, w_old_scales, w
         load_scales_old()
         load_w_old(1)
         load_w_old(2)
-        load_w_new(0)
         for i in range(4, 8):
             load_x(i)
+        load_w_new(0)
         load_w_new(1)
         load_w_new(2)
 
@@ -123,39 +123,46 @@ def tile_two_snapshot_sample_gram_s11_kernel(tc, x, w_old_words, w_old_scales, w
         def sort_x(i):
             x_sorted[i] = ring.tile([P, K // 2], F32, name="x_sorted", tag="x_sorted", bufs=4, align_bytes=64)
             nc.vector.tensor_copy(
-                out=x_sorted[i][:].rearrange("p (g u w) -> p g u w", g=KP, u=2),
-                in_=x_words[i].rearrange("p (g w u) -> p g u w", g=KP, u=2),
+                out=x_sorted[i][:].rearrange("p (u w) -> p u w", u=2),
+                in_=x_words[i].rearrange("p (w u) -> p u w", u=2),
             )
 
         turned = {}
 
-        def turn_x(h, pair, banks):
-            tiles = [bank(b) for b in banks]
-            turned[(h, pair)] = tiles
-            steps = [(a, g) for a in range(2) for g in range(KP)] if pair == 0 else [(a, g) for g in range(KP) for a in range(2)]
-            for a, g in steps:
-                if True:
-                    for u in range(2):
-                        col = (2 * a + u) * P
-                        i = 4 * h + 2 * pair + a
-                        if i in x_sorted:
-                            src = x_sorted[i][:, (2 * g + u) * P : (2 * g + u + 1) * P]
-                        else:
-                            src = x_words[i][:, g * 2 * P + u : (g + 1) * 2 * P : 2]
-                        nc.tensor.transpose(tiles[g][:, col : col + P], src, ident[:])
+        def turn_x(i, g, ps):
+            turned[(i, g)] = ps
+            for u in range(2):
+                col = (2 * (i % 2) + u) * P
+                if i in x_sorted:
+                    src = x_sorted[i][:, (KP * u + g) * P : (KP * u + g + 1) * P]
+                else:
+                    src = x_words[i][:, g * 2 * P + u : (g + 1) * 2 * P : 2]
+                nc.tensor.transpose(ps[:, col : col + P], src, ident[:])
 
-        def empty_x(h, pair, g, copy):
-            if pair == 0:
+        def empty_x(i, tiles, g, copy):
+            h, a = divmod(i, 4)
+            if a == 0:
                 x_grouped[(h, g)] = ring.tile([P, HALF * PACK], BF16, name="x_grouped", tag="x_grouped", align_bytes=64)
             words = x_grouped[(h, g)][:].bitcast(F32)
+            c0 = (i % 2) * 2 * P
             copy(
-                out=words[:, pair * HALF : (pair + 1) * HALF].rearrange("p (a r u) -> p a r u", a=2, u=2),
-                in_=turned[(h, pair)][g][:].rearrange("p (a u r) -> p a r u", a=2, u=2),
+                out=words[:, a * 2 * P : (a + tiles) * 2 * P].rearrange("p (a r u) -> p a r u", a=tiles, u=2),
+                in_=turned[(i, g)][:, c0 : c0 + tiles * 2 * P].rearrange("p (a u r) -> p a r u", a=tiles, u=2),
             )
 
         def quant_x(h, g):
             xq[(h, g)] = mx_pair("xq_%d_%d" % (h, g))
             quantize(xq[(h, g)], x_grouped[(h, g)])
+
+        def quant_x_half(h, g, part):
+            if part == 0:
+                xq[(h, g)] = mx_pair("xq_%d_%d" % (h, g))
+            codes, scales = xq[(h, g)]
+            cols = slice(part * HALF // 2, (part + 1) * HALF // 2)
+            nc.vector.quantize_mx(
+                out=codes[:, cols].bitcast(FP8X4), scales=scales[:, cols],
+                in_=x_grouped[(h, g)][:, part * HALF * 2 : (part + 1) * HALF * 2],
+            )
 
         neg_mean = kept("neg_mean", [P, PACK, 2 * NP], F32)
 
@@ -270,79 +277,89 @@ def tile_two_snapshot_sample_gram_s11_kernel(tc, x, w_old_words, w_old_scales, w
         low, high = range(4), range(4, 8)
         set_x, set_y = (0, 1, 2, 3), (4, 5, 6, 7)
         on_vector, on_scalar = nc.vector.tensor_copy, nc.scalar.copy
-        turn_x(0, 0, (0, 1, 2))
         nc.vector.tensor_scalar(
             out=neg_rows[0 : 2 * NP, :].rearrange("s (t a r) -> s t a r", t=PACK, r=4),
             in0=mean_rows[:].rearrange("s (a t r) -> s t a r", t=PACK, r=4),
             scalar1=-1.0, scalar2=None, op0=ALU.mult,
         )
-        empty_x(0, 0, 0, on_scalar)
-        empty_x(0, 0, 1, on_scalar)
-        empty_x(0, 0, 2, on_vector)
-        turn_x(0, 1, (4, 5, 6))
+        head = [bank(b) for b in range(KP)]
         for g in range(KP):
-            empty_x(0, 1, g, on_scalar)
+            turn_x(0, g, head[g])
+        for g in range(KP):
+            turn_x(1, g, head[g])
+        empty_x(0, 2, 0, on_scalar)
+        turn_x(2, 0, bank(3))
+        empty_x(2, 1, 0, on_scalar)
+        empty_x(0, 2, 1, on_scalar)
+        empty_x(0, 2, 2, on_vector)
+        quant_x_half(0, 0, 0)
+        turn_x(3, 0, bank(4))
+        empty_x(3, 1, 0, on_scalar)
+        for g in range(1, KP):
+            ps = bank(4 + g)
+            turn_x(2, g, ps)
+            turn_x(3, g, ps)
+            empty_x(2, 2, g, on_scalar)
         turn_means(7)
-        for g in range(KP):
+        sort_w_old(0)
+        quant_x_half(0, 0, 1)
+        sort_scales_old(0)
+        stage1_by_pass(OLD, 0, 0, 0, set_x)
+        for g in range(1, KP):
+            quant_x(0, g)
             sort_w_old(g)
             sort_scales_old(g)
-            quant_x(0, g)
             stage1_by_pass(OLD, 0, 0, g, set_x)
-        group_w(1, 0, 0, on_scalar)
+        for i in high:
+            sort_x(i)
         centre_all(OLD, 0, 0, set_x)
+        for pair, banks in ((2, (4, 5, 6)), (3, (7, 0, 1))):
+            tiles = [bank(b) for b in banks]
+            for g in range(KP):
+                turn_x(2 * pair, g, tiles[g])
+                turn_x(2 * pair + 1, g, tiles[g])
+        set_a, set_b = (5, 0, 6, 1), (2, 3, 4, 7)
+        empty_x(4, 2, 0, on_vector)
+        empty_x(4, 2, 1, on_vector)
+        empty_x(6, 2, 0, on_scalar)
+        empty_x(6, 2, 1, on_scalar)
+        empty_x(4, 2, 2, on_scalar)
+        empty_x(6, 2, 2, on_scalar)
         group_w(0, 0)
-        sort_x(4)
-        sort_x(5)
-        group_w(1, 0, 1)
-        sort_x(6)
+        for g in range(KP):
+            quant_x(1, g)
+        stage1_by_slot(OLD, 0, 1, low, set_b)
+        group_w(0, 1)
         quant(("w", 0, 0))
-        sort_x(7)
-        stage1_by_slot(OLD, 0, 1, (0, 1), (6, 7))
-        quant(("w", 1, 0))
-        turn_x(1, 0, (0, 2, 4))
-        turn_x(1, 1, (1, 3, 5))
-        stage1_slot(OLD, 0, 1, 2, 6)
-        stage1_slot(OLD, 0, 1, 3, 7)
-        group_ab(OLD, 0, 0, on_vector)
-        for g in range(KP):
-            empty_x(1, 0, g, on_scalar)
-            empty_x(1, 1, g, on_scalar)
-        quant(("a", 0, 0))
-        quant_x(1, 0)
-        group_w(0, 1, 0)
-        quant_x(1, 1)
-        group_w(0, 1, 1)
-        quant_x(1, 2)
-        centre(OLD, 0, 1, 2, 6)
-        centre(OLD, 0, 1, 3, 7)
-        for g in range(KP):
-            stage1_by_pass(OLD, 1, 0, g, set_x)
-        group_ab(OLD, 0, 1, on_scalar)
-        centre_all(OLD, 1, 0, set_x)
+        group_w(1, 0, None, on_scalar)
+        stage1_by_slot(OLD, 1, 0, low, set_a)
         group_w(0, 2)
         quant(("w", 0, 1))
         group_w(1, 1)
         quant(("w", 0, 2))
         group_w(1, 2)
-        quant(("w", 1, 1))
-        quant(("w", 1, 2))
-        quant(("a", 0, 1))
-        stage1_by_slot(OLD, 1, 1, low, set_y)
+        for g in range(KP):
+            quant(("w", 1, g))
+        stage1_by_slot(OLD, 1, 1, low, set_b)
         group_ab(OLD, 1, 0, on_vector)
-        stage1_by_slot(NEW, 0, 0, low, set_x)
+        group_ab(OLD, 0, 1, on_scalar)
         group_ab(OLD, 1, 1, on_vector)
         quant(("a", 1, 0))
-        group_ab(NEW, 0, 0, on_vector)
+        stage1_by_slot(NEW, 0, 0, low, set_a)
+        group_ab(OLD, 0, 0, on_vector)
         quant(("a", 1, 1))
-        quant(("b", 0, 0))
-        stage1_by_slot(NEW, 0, 1, low, set_y)
+        quant(("a", 0, 1))
+        group_ab(NEW, 0, 0, on_vector)
+        quant(("a", 0, 0))
+        stage1_by_slot(NEW, 0, 1, low, set_b)
         group_ab(NEW, 0, 1, on_vector)
+        quant(("b", 0, 0))
         quant(("b", 0, 1))
-        stage1_by_slot(NEW, 1, 0, low, set_x)
+        stage1_by_slot(NEW, 1, 0, low, set_a)
         group_ab(NEW, 1, 0, on_vector)
         quant(("b", 1, 0))
         order = [(4, 0), (5, 0), (6, 0), (7, 0), (0, 0), (1, 0), (2, 0), (3, 0), (4, 1), (5, 1), (0, 1), (6, 1), (1, 1), (7, 1), (2, 1), (3, 1)]
-        banks = list(range(8)) * 2
+        banks = (set_a + set_b) * 2
 
         def gram(step):
             i, h = order[step]
@@ -355,7 +372,7 @@ def tile_two_snapshot_sample_gram_s11_kernel(tc, x, w_old_words, w_old_scales, w
                 copy_out(i, h, b)
             store(i, h)
 
-        stage1_by_slot(NEW, 1, 1, low, set_y)
+        stage1_by_slot(NEW, 1, 1, low, set_b)
         group_ab(NEW, 1, 1, on_vector)
         quant(("b", 1, 1))
         for step in range(16):

@@ -23,6 +23,10 @@ PASS = P * PACK
 KP = K // PASS
 NP = N // PASS
 HALF = 512
+TILES = HALF // P
+RUN = 4
+WORDS = PASS // 2
+QUADRANT = 32
 OLD, NEW = 0, 1
 
 
@@ -30,9 +34,10 @@ def tile_two_snapshot_sample_gram_s11_kernel(tc, x, w_old_words, w_old_scales, w
     nc = tc.nc
     with ExitStack() as ctx:
         keep = ctx.enter_context(tc.tile_pool(name="keep", bufs=1))
-        ring = ctx.enter_context(tc.tile_pool(name="ring", bufs=3))
+        ring = ctx.enter_context(tc.tile_pool(name="ring", bufs=KP))
         psum = ctx.enter_context(tc.psum_pool(name="psum", bufs=1))
         ctx.enter_context(tc.manual_schedule())
+        on_vector, on_scalar = nc.vector.tensor_copy, nc.scalar.copy
 
         def kept(name, shape, dtype):
             return keep.tile(shape, dtype, name=name, tag=name, align_bytes=64)
@@ -40,11 +45,16 @@ def tile_two_snapshot_sample_gram_s11_kernel(tc, x, w_old_words, w_old_scales, w
         def bank(b):
             return psum.tile([P, HALF], F32, name="bank%d" % b, tag="bank%d" % b)
 
-        def mx_pair(name):
+        def mx_operand(name):
             return kept(name + "_codes", [P, HALF], U32), kept(name + "_scales", [P, HALF], U8)
 
-        def quantize(pair, grouped):
-            nc.vector.quantize_mx(out=pair[0][:].bitcast(FP8X4), scales=pair[1][:], in_=grouped[:])
+        def quantize(operand, source, first, count):
+            codes, scales = operand
+            nc.vector.quantize_mx(
+                out=codes[:, first : first + count].bitcast(FP8X4),
+                scales=scales[:, first : first + count],
+                in_=source[:, first * PACK : (first + count) * PACK],
+            )
 
         ident = kept("ident", [P, P], F32)
         make_identity(nc, ident[:])
@@ -58,13 +68,13 @@ def tile_two_snapshot_sample_gram_s11_kernel(tc, x, w_old_words, w_old_scales, w
         nc.scalar.activation(out=shift[:, HALF - P : HALF], in_=ident[:], func=ACT.Identity, bias=shift[:, 0:1], scale=EPS)
 
         x_words = {}
+        wo_raw = {}
+        wn_raw = {}
 
         def load_x(i):
-            t = kept("x_raw_%d" % i, [P, K], BF16)
-            nc.sync.dma_start(out=t[:], in_=x[i * P : (i + 1) * P, :])
-            x_words[i] = t[:].bitcast(F32)
-
-        wo_raw = {}
+            rows = kept("x_raw_%d" % i, [P, K], BF16)
+            nc.sync.dma_start(out=rows[:], in_=x[i * P : (i + 1) * P, :])
+            x_words[i] = rows[:].bitcast(F32)
 
         def load_w_old(g):
             wo_raw[g] = kept("wo_raw_%d" % g, [P, N // 2], I32)
@@ -74,31 +84,29 @@ def tile_two_snapshot_sample_gram_s11_kernel(tc, x, w_old_words, w_old_scales, w
         nc.vector.memset(so_raw[:], 0)
 
         def load_scales_old():
-            for r in range(4):
+            for j in range(4):
                 nc.sync.dma_start(
-                    out=so_raw[r:P:32, :].rearrange("q (g w) -> q g w", g=KP),
-                    in_=w_old_scales.bitcast(I32)[:, r:16:4, :].rearrange("g q w -> q g w"),
+                    out=so_raw[j:P:QUADRANT, :].rearrange("q (g w) -> q g w", g=KP),
+                    in_=w_old_scales.bitcast(I32)[:, j:16:4, :].rearrange("g q w -> q g w"),
                 )
-
-        wn_raw = {}
 
         def load_w_new(g):
             wn_raw[g] = kept("wn_raw_%d" % g, [P, PACK, N], BF16)
-            nc.sync.dma_start(out=wn_raw[g][:], in_=w_new[g * PASS : (g + 1) * PASS, :].rearrange("(p j) n -> p j n", j=PACK))
+            nc.sync.dma_start(out=wn_raw[g][:], in_=w_new[g * PASS : (g + 1) * PASS, :].rearrange("(p t) n -> p t n", t=PACK))
 
-        for i in range(4):
+        for i in range(TILES):
             load_x(i)
         load_w_old(0)
         load_scales_old()
-        load_w_old(1)
-        load_w_old(2)
-        for i in range(4, 8):
+        for g in range(1, KP):
+            load_w_old(g)
+        for i in range(TILES, 2 * TILES):
             load_x(i)
-        load_w_new(0)
-        load_w_new(1)
-        load_w_new(2)
+        for g in range(KP):
+            load_w_new(g)
 
         wo_codes = {}
+        wo_scales = kept("wo_scales", [P, KP * N], U8)
 
         def sort_w_old(g):
             wo_codes[g] = kept("wo_codes_%d" % g, [P, 2 * N], U8)
@@ -107,273 +115,235 @@ def tile_two_snapshot_sample_gram_s11_kernel(tc, x, w_old_words, w_old_scales, w
                 in_=wo_raw[g][:].rearrange("p (c a t w) -> p c t a w", c=NP, t=PACK, w=2),
             )
 
-        wo_scales = kept("wo_scales", [P, KP * N], U8)
-
         def sort_scales_old(g):
             nc.vector.tensor_copy(
                 out=wo_scales[:, g * N : (g + 1) * N].bitcast(I32).rearrange("p (c t a) -> p c t a", c=NP, t=PACK),
                 in_=so_raw[:, g * N // 4 : (g + 1) * N // 4].rearrange("p (c a t) -> p c t a", c=NP, t=PACK),
             )
 
-        x_grouped = {}
-        xq = {}
-
         x_sorted = {}
+        x_turned = {}
+        x_grouped = {}
+        x_mx = {}
 
         def sort_x(i):
-            x_sorted[i] = ring.tile([P, K // 2], F32, name="x_sorted", tag="x_sorted", bufs=4, align_bytes=64)
+            x_sorted[i] = ring.tile([P, K // 2], F32, name="x_sorted", tag="x_sorted", bufs=TILES, align_bytes=64)
             nc.vector.tensor_copy(
                 out=x_sorted[i][:].rearrange("p (u w) -> p u w", u=2),
                 in_=x_words[i].rearrange("p (w u) -> p u w", u=2),
             )
 
-        turned = {}
-
         def turn_x(i, g, ps):
-            turned[(i, g)] = ps
+            x_turned[(i, g)] = ps
             for u in range(2):
                 col = (2 * (i % 2) + u) * P
                 if i in x_sorted:
-                    src = x_sorted[i][:, (KP * u + g) * P : (KP * u + g + 1) * P]
+                    words = x_sorted[i][:, (KP * u + g) * P : (KP * u + g + 1) * P]
                 else:
-                    src = x_words[i][:, g * 2 * P + u : (g + 1) * 2 * P : 2]
-                nc.tensor.transpose(ps[:, col : col + P], src, ident[:])
+                    words = x_words[i][:, g * WORDS + u : (g + 1) * WORDS : 2]
+                nc.tensor.transpose(ps[:, col : col + P], words, ident[:])
 
-        def empty_x(i, tiles, g, copy):
-            h, a = divmod(i, 4)
-            if a == 0:
+        def empty_x(i, count, g, copy):
+            h, first = divmod(i, TILES)
+            if first == 0:
                 x_grouped[(h, g)] = ring.tile([P, HALF * PACK], BF16, name="x_grouped", tag="x_grouped", align_bytes=64)
-            words = x_grouped[(h, g)][:].bitcast(F32)
-            c0 = (i % 2) * 2 * P
+            col = (i % 2) * 2 * P
             copy(
-                out=words[:, a * 2 * P : (a + tiles) * 2 * P].rearrange("p (a r u) -> p a r u", a=tiles, u=2),
-                in_=turned[(i, g)][:, c0 : c0 + tiles * 2 * P].rearrange("p (a u r) -> p a r u", a=tiles, u=2),
+                out=x_grouped[(h, g)][:].bitcast(F32)[:, first * 2 * P : (first + count) * 2 * P].rearrange("p (i m u) -> p i m u", i=count, u=2),
+                in_=x_turned[(i, g)][:, col : col + count * 2 * P].rearrange("p (i u m) -> p i m u", i=count, u=2),
             )
 
-        def quant_x(h, g):
-            xq[(h, g)] = mx_pair("xq_%d_%d" % (h, g))
-            quantize(xq[(h, g)], x_grouped[(h, g)])
-
-        def quant_x_half(h, g, part):
-            if part == 0:
-                xq[(h, g)] = mx_pair("xq_%d_%d" % (h, g))
-            codes, scales = xq[(h, g)]
-            cols = slice(part * HALF // 2, (part + 1) * HALF // 2)
-            nc.vector.quantize_mx(
-                out=codes[:, cols].bitcast(FP8X4), scales=scales[:, cols],
-                in_=x_grouped[(h, g)][:, part * HALF * 2 : (part + 1) * HALF * 2],
-            )
+        def quant_x(h, g, first=0, count=HALF):
+            if first == 0:
+                x_mx[(h, g)] = mx_operand("xq_%d_%d" % (h, g))
+            quantize(x_mx[(h, g)], x_grouped[(h, g)], first, count)
 
         neg_mean = kept("neg_mean", [P, PACK, 2 * NP], F32)
+
+        def negate_means():
+            nc.vector.tensor_scalar(
+                out=neg_rows[0 : 2 * NP, :].rearrange("s (t a r) -> s t a r", t=PACK, r=RUN),
+                in0=mean_rows[:].rearrange("s (a t r) -> s t a r", t=PACK, r=RUN),
+                scalar1=-1.0, scalar2=None, op0=ALU.mult,
+            )
 
         def turn_means(b):
             ps = bank(b)
             for t in range(PACK):
                 nc.tensor.transpose(ps[:, t * P : (t + 1) * P], neg_rows[:, t * P : (t + 1) * P], ident[:])
-            nc.scalar.copy(out=neg_mean[:], in_=ps[:].rearrange("p (t r) -> p t r", t=PACK)[:, :, 0 : 2 * NP])
+            nc.scalar.copy(out=neg_mean[:], in_=ps[:].rearrange("p (t row) -> p t row", t=PACK)[:, :, 0 : 2 * NP])
 
         grouped = {}
         quantized = {}
+        centred = {}
 
         def new_grouped(key):
             grouped[key] = ring.tile([P, HALF * PACK], BF16, name="grouped", tag="grouped", bufs=4, align_bytes=64)
             return grouped[key]
 
-        def group_w(c, g, part=None, copy=nc.vector.tensor_copy):
-            if part in (None, 0):
-                new_grouped(("w", c, g))
-            cols = slice(0, 32) if part is None else slice(16 * part, 16 * (part + 1))
+        def group_w(c, g, copy):
             copy(
-                out=grouped[("w", c, g)][:].rearrange("p (t a r j) -> p a t j r", t=PACK, r=4, j=PACK)[:, cols],
-                in_=wn_raw[g][:, :, c * PASS : (c + 1) * PASS].rearrange("p j (a t r) -> p a t j r", t=PACK, r=4)[:, cols],
+                out=new_grouped(("w", c, g))[:].rearrange("p (t a r j) -> p a t j r", t=PACK, r=RUN, j=PACK),
+                in_=wn_raw[g][:, :, c * PASS : (c + 1) * PASS].rearrange("p j (a t r) -> p a t j r", t=PACK, r=RUN),
+            )
+
+        def group_ab(s, h, c, copy):
+            copy(
+                out=new_grouped(("ab"[s], h, c))[:].rearrange("p (m e t) -> p m t e", e=4, t=PACK),
+                in_=centred[(s, h, c)][:].rearrange("p t (m e) -> p m t e", e=4),
             )
 
         def quant(key):
-            quantized[key] = mx_pair("q_%s_%d_%d" % (key[0], key[1], key[2]))
-            quantize(quantized[key], grouped[key])
+            quantized[key] = mx_operand("q_%s_%d_%d" % key)
+            quantize(quantized[key], grouped[key], 0, HALF)
 
-        open_banks = {}
-        centred = {}
+        sums = {}
 
         def stage1_pass(s, h, c, t, g, b):
             if g == 0:
-                open_banks[b] = bank(b)
-            cols = slice(t * P, (t + 1) * P)
+                sums[b] = bank(b)
             if s == OLD:
-                c0 = c * PASS + t * P
-                lhsT = wo_codes[g][:, 2 * c0 : 2 * (c0 + P)].bitcast(FP4X4)
-                lhsT_scale = wo_scales[:, g * N + c0 : g * N + c0 + P]
+                col = c * PASS + t * P
+                lhsT = wo_codes[g][:, 2 * col : 2 * (col + P)].bitcast(FP4X4)
+                lhsT_scale = wo_scales[:, g * N + col : g * N + col + P]
             else:
-                lhsT = quantized[("w", c, g)][0][:, cols].bitcast(FP8X4)
-                lhsT_scale = quantized[("w", c, g)][1][:, cols]
+                codes, scales = quantized[("w", c, g)]
+                lhsT = codes[:, t * P : (t + 1) * P].bitcast(FP8X4)
+                lhsT_scale = scales[:, t * P : (t + 1) * P]
             nc.tensor.matmul_mx(
-                out=open_banks[b][:], lhsT=lhsT, lhsT_scale=lhsT_scale,
-                rhs=xq[(h, g)][0][:].bitcast(FP8X4), rhs_scale=xq[(h, g)][1][:],
+                out=sums[b][:], lhsT=lhsT, lhsT_scale=lhsT_scale,
+                rhs=x_mx[(h, g)][0][:].bitcast(FP8X4), rhs_scale=x_mx[(h, g)][1][:],
                 start=(g == 0), stop=(g == KP - 1),
             )
-
-        def centre(s, h, c, t, b):
-            if t == 0:
-                centred[(s, h, c)] = kept("centred_%d_%d_%d" % (s, h, c), [P, PACK, HALF], BF16)
-            nc.scalar.activation(
-                out=centred[(s, h, c)][:, t, :], in_=open_banks[b][:], func=ACT.Identity,
-                bias=neg_mean[:, t, NP * s + c : NP * s + c + 1], scale=1.0,
-            )
-
-        def stage1_by_pass(s, h, c, g, banks):
-            for t in range(PACK):
-                stage1_pass(s, h, c, t, g, banks[t])
-
-        def centre_all(s, h, c, banks):
-            for t in range(PACK):
-                centre(s, h, c, t, banks[t])
 
         def stage1_slot(s, h, c, t, b):
             for g in range(KP):
                 stage1_pass(s, h, c, t, g, b)
 
-        def stage1_by_slot(s, h, c, slots, banks):
-            for t, b in zip(slots, banks):
-                stage1_slot(s, h, c, t, b)
-                centre(s, h, c, t, b)
-
-        def group_ab(s, h, c, copy):
-            dst = new_grouped(("ab"[s], h, c))
-            copy(
-                out=dst[:].rearrange("p (a i t) -> p a t i", i=4, t=PACK),
-                in_=centred[(s, h, c)][:].rearrange("p t (a i) -> p a t i", i=4),
+        def centre(s, h, c, t, b):
+            if t == 0:
+                centred[(s, h, c)] = kept("centred_%d_%d_%d" % (s, h, c), [P, PACK, HALF], BF16)
+            nc.scalar.activation(
+                out=centred[(s, h, c)][:, t, :], in_=sums[b][:], func=ACT.Identity,
+                bias=neg_mean[:, t, NP * s + c : NP * s + c + 1], scale=1.0,
             )
 
-        def gram_pass(i, h, c, b):
-            if c == 0:
-                open_banks[b] = bank(b)
-            a_codes, a_scales = quantized[("a", i // 4, c)]
-            b_codes, b_scales = quantized[("b", h, c)]
-            cols = slice((i % 4) * P, (i % 4 + 1) * P)
-            nc.tensor.matmul_mx(
-                out=open_banks[b][:], lhsT=a_codes[:, cols].bitcast(FP8X4), lhsT_scale=a_scales[:, cols],
-                rhs=b_codes[:].bitcast(FP8X4), rhs_scale=b_scales[:],
-                start=(c == 0), stop=(c == NP - 1),
-            )
+        def stage1_group(s, h, c, banks, first_slot=0):
+            for t in range(first_slot, PACK):
+                stage1_slot(s, h, c, t, banks[t])
+                centre(s, h, c, t, banks[t])
 
-        result = {}
+        def gram_tile(i, h, b):
+            ps = bank(b)
+            block = i % TILES
+            for c in range(NP):
+                a_codes, a_scales = quantized[("a", i // TILES, c)]
+                b_codes, b_scales = quantized[("b", h, c)]
+                nc.tensor.matmul_mx(
+                    out=ps[:],
+                    lhsT=a_codes[:, block * P : (block + 1) * P].bitcast(FP8X4),
+                    lhsT_scale=a_scales[:, block * P : (block + 1) * P],
+                    rhs=b_codes[:].bitcast(FP8X4), rhs_scale=b_scales[:],
+                    start=(c == 0), stop=(c == NP - 1),
+                )
+            result = kept("result_%d_%d" % (i, h), [P, HALF], F32)
+            if i // TILES == h:
+                col = HALF - P - block * P
+                nc.vector.tensor_tensor(out=result[:], in0=ps[:], in1=shift[:, col : col + HALF], op=ALU.mult)
+            else:
+                nc.scalar.copy(out=result[:], in_=ps[:])
+            nc.sync.dma_start(out=out[i * P : (i + 1) * P, h * HALF : (h + 1) * HALF], in_=result[:])
 
-        def store(i, h):
-            nc.sync.dma_start(out=out[i * P : (i + 1) * P, h * HALF : (h + 1) * HALF], in_=result[(i, h)][:])
-
-        def copy_out(i, h, b):
-            result[(i, h)] = kept("result_%d_%d" % (i, h), [P, HALF], F32)
-            nc.scalar.copy(out=result[(i, h)][:], in_=open_banks[b][:])
-
-        def shift_in_place(i, h):
-            cols = slice((i % 4) * P, (i % 4 + 1) * P)
-            nc.vector.tensor_tensor(out=result[(i, h)][:, cols], in0=result[(i, h)][:, cols], in1=shift[:, HALF - P : HALF], op=ALU.mult)
-
-        def shifted_out(i, h, b):
-            result[(i, h)] = kept("result_%d_%d" % (i, h), [P, HALF], F32)
-            c0 = HALF - P - (i % 4) * P
-            nc.vector.tensor_tensor(out=result[(i, h)][:], in0=open_banks[b][:], in1=shift[:, c0 : c0 + HALF], op=ALU.mult)
-
-        low, high = range(4), range(4, 8)
-        set_x, set_y = (0, 1, 2, 3), (4, 5, 6, 7)
-        on_vector, on_scalar = nc.vector.tensor_copy, nc.scalar.copy
-        nc.vector.tensor_scalar(
-            out=neg_rows[0 : 2 * NP, :].rearrange("s (t a r) -> s t a r", t=PACK, r=4),
-            in0=mean_rows[:].rearrange("s (a t r) -> s t a r", t=PACK, r=4),
-            scalar1=-1.0, scalar2=None, op0=ALU.mult,
-        )
-        head = [bank(b) for b in range(KP)]
-        for g in range(KP):
-            turn_x(0, g, head[g])
-        for g in range(KP):
-            turn_x(1, g, head[g])
+        negate_means()
+        first_pair = [bank(g) for g in range(KP)]
+        for i in range(2):
+            for g in range(KP):
+                turn_x(i, g, first_pair[g])
         empty_x(0, 2, 0, on_scalar)
-        turn_x(2, 0, bank(3))
-        empty_x(2, 1, 0, on_scalar)
-        empty_x(0, 2, 1, on_scalar)
-        empty_x(0, 2, 2, on_vector)
-        quant_x_half(0, 0, 0)
-        turn_x(3, 0, bank(4))
-        empty_x(3, 1, 0, on_scalar)
+        for i in (2, 3):
+            turn_x(i, 0, bank(i + 1))
+            empty_x(i, 1, 0, on_scalar)
+        for g in range(1, KP):
+            empty_x(0, 2, g, on_vector)
+        quant_x(0, 0, 0, HALF // 2)
         for g in range(1, KP):
             ps = bank(4 + g)
             turn_x(2, g, ps)
             turn_x(3, g, ps)
             empty_x(2, 2, g, on_scalar)
         turn_means(7)
+
         sort_w_old(0)
-        quant_x_half(0, 0, 1)
-        sort_scales_old(0)
-        stage1_by_pass(OLD, 0, 0, 0, set_x)
-        for g in range(1, KP):
-            quant_x(0, g)
-            sort_w_old(g)
+        quant_x(0, 0, HALF // 2, HALF // 2)
+        for g in range(KP):
+            if g > 0:
+                quant_x(0, g)
+                sort_w_old(g)
             sort_scales_old(g)
-            stage1_by_pass(OLD, 0, 0, g, set_x)
-        for i in high:
+            for t in range(PACK):
+                stage1_pass(OLD, 0, 0, t, g, t)
+        for i in range(TILES, 2 * TILES):
             sort_x(i)
-        centre_all(OLD, 0, 0, set_x)
-        for pair, banks in ((2, (4, 5, 6)), (3, (7, 0, 1))):
-            tiles = [bank(b) for b in banks]
+        for t in range(PACK):
+            centre(OLD, 0, 0, t, t)
+
+        def turn_pair(i, first_bank):
+            tiles = [bank(first_bank + g) for g in range(KP)]
             for g in range(KP):
-                turn_x(2 * pair, g, tiles[g])
-                turn_x(2 * pair + 1, g, tiles[g])
-        set_a, set_b = (5, 0, 6, 1), (2, 3, 4, 7)
+                turn_x(i, g, tiles[g])
+                turn_x(i + 1, g, tiles[g])
+
+        banks_odd, banks_even = (7, 3, 4, 0), (5, 1, 6, 2)
+        turn_pair(4, 4)
+        stage1_slot(OLD, 0, 1, 0, banks_odd[0])
+        turn_pair(6, 0)
         empty_x(4, 2, 0, on_vector)
         empty_x(4, 2, 1, on_vector)
-        empty_x(6, 2, 0, on_scalar)
-        empty_x(6, 2, 1, on_scalar)
         empty_x(4, 2, 2, on_scalar)
-        empty_x(6, 2, 2, on_scalar)
-        group_w(0, 0)
+        centre(OLD, 0, 1, 0, banks_odd[0])
+        for g in range(KP):
+            empty_x(6, 2, g, on_scalar)
+        group_w(0, 0, on_vector)
         for g in range(KP):
             quant_x(1, g)
-        stage1_by_slot(OLD, 0, 1, low, set_b)
-        group_w(0, 1)
+        stage1_group(OLD, 0, 1, banks_odd, first_slot=1)
+
+        group_w(0, 1, on_vector)
         quant(("w", 0, 0))
-        group_w(1, 0, None, on_scalar)
-        stage1_by_slot(OLD, 1, 0, low, set_a)
-        group_w(0, 2)
+        group_w(1, 0, on_scalar)
+        stage1_group(OLD, 1, 0, banks_even)
+        group_w(0, 2, on_vector)
         quant(("w", 0, 1))
-        group_w(1, 1)
+        group_w(1, 1, on_vector)
         quant(("w", 0, 2))
-        group_w(1, 2)
+        group_w(1, 2, on_vector)
         for g in range(KP):
             quant(("w", 1, g))
-        stage1_by_slot(OLD, 1, 1, low, set_b)
+        stage1_group(OLD, 1, 1, banks_odd)
+
         group_ab(OLD, 1, 0, on_vector)
         group_ab(OLD, 0, 1, on_scalar)
         group_ab(OLD, 1, 1, on_vector)
         quant(("a", 1, 0))
-        stage1_by_slot(NEW, 0, 0, low, set_a)
+        stage1_group(NEW, 0, 0, banks_even)
         group_ab(OLD, 0, 0, on_vector)
         quant(("a", 1, 1))
         quant(("a", 0, 1))
         group_ab(NEW, 0, 0, on_vector)
         quant(("a", 0, 0))
-        stage1_by_slot(NEW, 0, 1, low, set_b)
+        stage1_group(NEW, 0, 1, banks_odd)
         group_ab(NEW, 0, 1, on_vector)
         quant(("b", 0, 0))
         quant(("b", 0, 1))
-        stage1_by_slot(NEW, 1, 0, low, set_a)
-        group_ab(NEW, 1, 0, on_vector)
-        quant(("b", 1, 0))
-        order = [(4, 0), (5, 0), (6, 0), (7, 0), (0, 0), (1, 0), (2, 0), (3, 0), (4, 1), (5, 1), (0, 1), (6, 1), (1, 1), (7, 1), (2, 1), (3, 1)]
-        banks = (set_a + set_b) * 2
+        for c, banks in enumerate((banks_even, banks_odd)):
+            stage1_group(NEW, 1, c, banks)
+            group_ab(NEW, 1, c, on_vector)
+            quant(("b", 1, c))
 
-        def gram(step):
-            i, h = order[step]
-            b = banks[step]
-            for c in range(NP):
-                gram_pass(i, h, c, b)
-            if i // 4 == h:
-                shifted_out(i, h, b)
-            else:
-                copy_out(i, h, b)
-            store(i, h)
-
-        stage1_by_slot(NEW, 1, 1, low, set_b)
-        group_ab(NEW, 1, 1, on_vector)
-        quant(("b", 1, 1))
-        for step in range(16):
-            gram(step)
+        low, high = list(range(TILES)), list(range(TILES, 2 * TILES))
+        order = [(i, 0) for i in high + low] + [(i, 1) for i in high[:2]]
+        for off_diagonal, diagonal in zip(low[:2], high[2:]):
+            order = order + [(off_diagonal, 1), (diagonal, 1)]
+        order = order + [(i, 1) for i in low[2:]]
+        for (i, h), b in zip(order, (banks_even + banks_odd) * 2):
+            gram_tile(i, h, b)

from contextlib import ExitStack

import concourse.mybir as mybir
from concourse.masks import make_identity

M, K, N = 1024, 1536, 1024
EPS = 0.1
FLOPS = 2 * (2 * M * K * N) + 2 * M * M * N

F32 = mybir.dt.float32
BF16 = mybir.dt.bfloat16
I32 = mybir.dt.int32
U32 = mybir.dt.uint32
U8 = mybir.dt.uint8
FP8X4 = mybir.dt.float8_e4m3fn_x4
FP4X4 = mybir.dt.float4_e2m1fn_x4
ALU = mybir.AluOpType
ACT = mybir.ActivationFunctionType

P = 128
PACK = 4
PASS = P * PACK
KP = K // PASS
NP = N // PASS
HALF = 512
TILES = HALF // P
RUN = 4
WORDS = PASS // 2
QUADRANT = 32
OLD, NEW = 0, 1


def tile_two_snapshot_sample_gram_s11_kernel(tc, x, w_old_words, w_old_scales, w_new, mean_old, mean_new, out):
    nc = tc.nc
    with ExitStack() as ctx:
        keep = ctx.enter_context(tc.tile_pool(name="keep", bufs=1))
        ring = ctx.enter_context(tc.tile_pool(name="ring", bufs=KP))
        psum = ctx.enter_context(tc.psum_pool(name="psum", bufs=1))
        ctx.enter_context(tc.manual_schedule())
        on_vector, on_scalar = nc.vector.tensor_copy, nc.scalar.copy

        def kept(name, shape, dtype):
            return keep.tile(shape, dtype, name=name, tag=name, align_bytes=64)

        def bank(b):
            return psum.tile([P, HALF], F32, name="bank%d" % b, tag="bank%d" % b)

        def mx_operand(name):
            return kept(name + "_codes", [P, HALF], U32), kept(name + "_scales", [P, HALF], U8)

        def quantize(operand, source, first, count):
            codes, scales = operand
            nc.vector.quantize_mx(
                out=codes[:, first : first + count].bitcast(FP8X4),
                scales=scales[:, first : first + count],
                in_=source[:, first * PACK : (first + count) * PACK],
            )

        ident = kept("ident", [P, P], F32)
        make_identity(nc, ident[:])
        shift = kept("shift", [P, 2 * HALF - P], F32)
        nc.gpsimd.memset(shift[:], 1.0)
        neg_rows = kept("neg_rows", [P, PASS], F32)
        nc.vector.memset(neg_rows[:], 0.0)
        mean_rows = kept("mean_rows", [2 * NP, PASS], BF16)
        for s, mean in ((OLD, mean_old), (NEW, mean_new)):
            nc.scalar.dma_start(out=mean_rows[NP * s : NP * (s + 1), :], in_=mean.rearrange("(c n) -> c n", c=NP))
        nc.scalar.activation(out=shift[:, HALF - P : HALF], in_=ident[:], func=ACT.Identity, bias=shift[:, 0:1], scale=EPS)

        x_words = {}
        wo_raw = {}
        wn_raw = {}

        def load_x(i):
            rows = kept("x_raw_%d" % i, [P, K], BF16)
            nc.sync.dma_start(out=rows[:], in_=x[i * P : (i + 1) * P, :])
            x_words[i] = rows[:].bitcast(F32)

        def load_w_old(g):
            wo_raw[g] = kept("wo_raw_%d" % g, [P, N // 2], I32)
            nc.sync.dma_start(out=wo_raw[g][:], in_=w_old_words[g].bitcast(I32))

        so_raw = kept("so_raw", [P, KP * N // 4], I32)
        nc.vector.memset(so_raw[:], 0)

        def load_scales_old():
            for j in range(4):
                nc.sync.dma_start(
                    out=so_raw[j:P:QUADRANT, :].rearrange("q (g w) -> q g w", g=KP),
                    in_=w_old_scales.bitcast(I32)[:, j:16:4, :].rearrange("g q w -> q g w"),
                )

        def load_w_new(g):
            wn_raw[g] = kept("wn_raw_%d" % g, [P, PACK, N], BF16)
            nc.sync.dma_start(out=wn_raw[g][:], in_=w_new[g * PASS : (g + 1) * PASS, :].rearrange("(p t) n -> p t n", t=PACK))

        for i in range(TILES):
            load_x(i)
        load_w_old(0)
        load_scales_old()
        for g in range(1, KP):
            load_w_old(g)
        for i in range(TILES, 2 * TILES):
            load_x(i)
        for g in range(KP):
            load_w_new(g)

        wo_codes = {}
        wo_scales = kept("wo_scales", [P, KP * N], U8)

        def sort_w_old(g):
            wo_codes[g] = kept("wo_codes_%d" % g, [P, 2 * N], U8)
            nc.vector.tensor_copy(
                out=wo_codes[g][:].bitcast(I32).rearrange("p (c t a w) -> p c t a w", c=NP, t=PACK, w=2),
                in_=wo_raw[g][:].rearrange("p (c a t w) -> p c t a w", c=NP, t=PACK, w=2),
            )

        def sort_scales_old(g):
            nc.vector.tensor_copy(
                out=wo_scales[:, g * N : (g + 1) * N].bitcast(I32).rearrange("p (c t a) -> p c t a", c=NP, t=PACK),
                in_=so_raw[:, g * N // 4 : (g + 1) * N // 4].rearrange("p (c a t) -> p c t a", c=NP, t=PACK),
            )

        x_sorted = {}
        x_turned = {}
        x_grouped = {}
        x_mx = {}

        def sort_x(i):
            x_sorted[i] = ring.tile([P, K // 2], F32, name="x_sorted", tag="x_sorted", bufs=TILES, align_bytes=64)
            nc.vector.tensor_copy(
                out=x_sorted[i][:].rearrange("p (u w) -> p u w", u=2),
                in_=x_words[i].rearrange("p (w u) -> p u w", u=2),
            )

        def turn_x(i, g, ps):
            x_turned[(i, g)] = ps
            for u in range(2):
                col = (2 * (i % 2) + u) * P
                if i in x_sorted:
                    words = x_sorted[i][:, (KP * u + g) * P : (KP * u + g + 1) * P]
                else:
                    words = x_words[i][:, g * WORDS + u : (g + 1) * WORDS : 2]
                nc.tensor.transpose(ps[:, col : col + P], words, ident[:])

        def empty_x(i, count, g, copy):
            h, first = divmod(i, TILES)
            if first == 0:
                x_grouped[(h, g)] = ring.tile([P, HALF * PACK], BF16, name="x_grouped", tag="x_grouped", align_bytes=64)
            col = (i % 2) * 2 * P
            copy(
                out=x_grouped[(h, g)][:].bitcast(F32)[:, first * 2 * P : (first + count) * 2 * P].rearrange("p (i m u) -> p i m u", i=count, u=2),
                in_=x_turned[(i, g)][:, col : col + count * 2 * P].rearrange("p (i u m) -> p i m u", i=count, u=2),
            )

        def quant_x(h, g, first=0, count=HALF):
            if first == 0:
                x_mx[(h, g)] = mx_operand("xq_%d_%d" % (h, g))
            quantize(x_mx[(h, g)], x_grouped[(h, g)], first, count)

        neg_mean = kept("neg_mean", [P, PACK, 2 * NP], F32)

        def negate_means():
            nc.vector.tensor_scalar(
                out=neg_rows[0 : 2 * NP, :].rearrange("s (t a r) -> s t a r", t=PACK, r=RUN),
                in0=mean_rows[:].rearrange("s (a t r) -> s t a r", t=PACK, r=RUN),
                scalar1=-1.0, scalar2=None, op0=ALU.mult,
            )

        def turn_means(b):
            ps = bank(b)
            for t in range(PACK):
                nc.tensor.transpose(ps[:, t * P : (t + 1) * P], neg_rows[:, t * P : (t + 1) * P], ident[:])
            nc.scalar.copy(out=neg_mean[:], in_=ps[:].rearrange("p (t row) -> p t row", t=PACK)[:, :, 0 : 2 * NP])

        grouped = {}
        quantized = {}
        centred = {}

        def new_grouped(key):
            grouped[key] = ring.tile([P, HALF * PACK], BF16, name="grouped", tag="grouped", bufs=4, align_bytes=64)
            return grouped[key]

        def group_w(c, g, copy):
            copy(
                out=new_grouped(("w", c, g))[:].rearrange("p (t a r j) -> p a t j r", t=PACK, r=RUN, j=PACK),
                in_=wn_raw[g][:, :, c * PASS : (c + 1) * PASS].rearrange("p j (a t r) -> p a t j r", t=PACK, r=RUN),
            )

        def group_ab(s, h, c, copy):
            copy(
                out=new_grouped(("ab"[s], h, c))[:].rearrange("p (m e t) -> p m t e", e=4, t=PACK),
                in_=centred[(s, h, c)][:].rearrange("p t (m e) -> p m t e", e=4),
            )

        def quant(key):
            quantized[key] = mx_operand("q_%s_%d_%d" % key)
            quantize(quantized[key], grouped[key], 0, HALF)

        sums = {}

        def stage1_pass(s, h, c, t, g, b):
            if g == 0:
                sums[b] = bank(b)
            if s == OLD:
                col = c * PASS + t * P
                lhsT = wo_codes[g][:, 2 * col : 2 * (col + P)].bitcast(FP4X4)
                lhsT_scale = wo_scales[:, g * N + col : g * N + col + P]
            else:
                codes, scales = quantized[("w", c, g)]
                lhsT = codes[:, t * P : (t + 1) * P].bitcast(FP8X4)
                lhsT_scale = scales[:, t * P : (t + 1) * P]
            nc.tensor.matmul_mx(
                out=sums[b][:], lhsT=lhsT, lhsT_scale=lhsT_scale,
                rhs=x_mx[(h, g)][0][:].bitcast(FP8X4), rhs_scale=x_mx[(h, g)][1][:],
                start=(g == 0), stop=(g == KP - 1),
            )

        def stage1_slot(s, h, c, t, b):
            for g in range(KP):
                stage1_pass(s, h, c, t, g, b)

        def centre(s, h, c, t, b):
            if t == 0:
                centred[(s, h, c)] = kept("centred_%d_%d_%d" % (s, h, c), [P, PACK, HALF], BF16)
            nc.scalar.activation(
                out=centred[(s, h, c)][:, t, :], in_=sums[b][:], func=ACT.Identity,
                bias=neg_mean[:, t, NP * s + c : NP * s + c + 1], scale=1.0,
            )

        def stage1_group(s, h, c, banks, first_slot=0):
            for t in range(first_slot, PACK):
                stage1_slot(s, h, c, t, banks[t])
                centre(s, h, c, t, banks[t])

        def gram_tile(i, h, b):
            ps = bank(b)
            block = i % TILES
            for c in range(NP):
                a_codes, a_scales = quantized[("a", i // TILES, c)]
                b_codes, b_scales = quantized[("b", h, c)]
                nc.tensor.matmul_mx(
                    out=ps[:],
                    lhsT=a_codes[:, block * P : (block + 1) * P].bitcast(FP8X4),
                    lhsT_scale=a_scales[:, block * P : (block + 1) * P],
                    rhs=b_codes[:].bitcast(FP8X4), rhs_scale=b_scales[:],
                    start=(c == 0), stop=(c == NP - 1),
                )
            result = kept("result_%d_%d" % (i, h), [P, HALF], F32)
            if i // TILES == h:
                col = HALF - P - block * P
                nc.vector.tensor_tensor(out=result[:], in0=ps[:], in1=shift[:, col : col + HALF], op=ALU.mult)
            else:
                nc.scalar.copy(out=result[:], in_=ps[:])
            nc.sync.dma_start(out=out[i * P : (i + 1) * P, h * HALF : (h + 1) * HALF], in_=result[:])

        negate_means()
        first_pair = [bank(g) for g in range(KP)]
        for i in range(2):
            for g in range(KP):
                turn_x(i, g, first_pair[g])
        empty_x(0, 2, 0, on_scalar)
        for i in (2, 3):
            turn_x(i, 0, bank(i + 1))
            empty_x(i, 1, 0, on_scalar)
        for g in range(1, KP):
            empty_x(0, 2, g, on_vector)
        quant_x(0, 0, 0, HALF // 2)
        for g in range(1, KP):
            ps = bank(4 + g)
            turn_x(2, g, ps)
            turn_x(3, g, ps)
            empty_x(2, 2, g, on_scalar)
        turn_means(7)

        sort_w_old(0)
        quant_x(0, 0, HALF // 2, HALF // 2)
        for g in range(KP):
            if g > 0:
                quant_x(0, g)
                sort_w_old(g)
            sort_scales_old(g)
            for t in range(PACK):
                stage1_pass(OLD, 0, 0, t, g, t)
        for i in range(TILES, 2 * TILES):
            sort_x(i)
        for t in range(PACK):
            centre(OLD, 0, 0, t, t)

        def turn_pair(i, first_bank):
            tiles = [bank(first_bank + g) for g in range(KP)]
            for g in range(KP):
                turn_x(i, g, tiles[g])
                turn_x(i + 1, g, tiles[g])

        banks_odd, banks_even = (7, 3, 4, 0), (5, 1, 6, 2)
        turn_pair(4, 4)
        stage1_slot(OLD, 0, 1, 0, banks_odd[0])
        turn_pair(6, 0)
        empty_x(4, 2, 0, on_vector)
        empty_x(4, 2, 1, on_vector)
        empty_x(4, 2, 2, on_scalar)
        centre(OLD, 0, 1, 0, banks_odd[0])
        for g in range(KP):
            empty_x(6, 2, g, on_scalar)
        group_w(0, 0, on_vector)
        for g in range(KP):
            quant_x(1, g)
        stage1_group(OLD, 0, 1, banks_odd, first_slot=1)

        group_w(0, 1, on_vector)
        quant(("w", 0, 0))
        group_w(1, 0, on_scalar)
        stage1_group(OLD, 1, 0, banks_even)
        group_w(0, 2, on_vector)
        quant(("w", 0, 1))
        group_w(1, 1, on_vector)
        quant(("w", 0, 2))
        group_w(1, 2, on_vector)
        for g in range(KP):
            quant(("w", 1, g))
        stage1_group(OLD, 1, 1, banks_odd)

        group_ab(OLD, 1, 0, on_vector)
        group_ab(OLD, 0, 1, on_scalar)
        group_ab(OLD, 1, 1, on_vector)
        quant(("a", 1, 0))
        stage1_group(NEW, 0, 0, banks_even)
        group_ab(OLD, 0, 0, on_vector)
        quant(("a", 1, 1))
        quant(("a", 0, 1))
        group_ab(NEW, 0, 0, on_vector)
        quant(("a", 0, 0))
        stage1_group(NEW, 0, 1, banks_odd)
        group_ab(NEW, 0, 1, on_vector)
        quant(("b", 0, 0))
        quant(("b", 0, 1))
        for c, banks in enumerate((banks_even, banks_odd)):
            stage1_group(NEW, 1, c, banks)
            group_ab(NEW, 1, c, on_vector)
            quant(("b", 1, c))

        low, high = list(range(TILES)), list(range(TILES, 2 * TILES))
        order = [(i, 0) for i in high + low] + [(i, 1) for i in high[:2]]
        for off_diagonal, diagonal in zip(low[:2], high[2:]):
            order = order + [(off_diagonal, 1), (diagonal, 1)]
        order = order + [(i, 1) for i in low[2:]]
        for (i, h), b in zip(order, (banks_even + banks_odd) * 2):
            gram_tile(i, h, b)
